import numpy as np
CORES = [6,14,22,30,38,46,54,62,70,78,86,94,102,110,118,126,134,142,150,158,166,174,182,190,198,206,214,222,230,238,246,254]
N = 32
TOK, D = 32, 512
ROUTE = [[[21,25],[12,23],[4,9],[0,23],[21,25],[5,24],[2,17],[10,21],[4,5],[22,28],[11,24],[15,19],[16,24],[9,24],[5,19],[3,31],[5,14],[12,16],[25,29],[7,10],[10,23],[0,16],[3,23],[5,10],[9,26],[15,31],[3,4],[14,22],[24,25],[16,18],[28,30],[8,9]],[[9,26],[6,24],[10,22],[4,14],[0,11],[9,17],[3,6],[4,9],[1,2],[1,11],[9,16],[4,10],[3,22],[4,16],[16,27],[3,18],[18,26],[0,15],[0,13],[7,18],[10,20],[7,31],[21,23],[11,25],[24,25],[0,24],[18,19],[6,23],[4,28],[13,31],[19,30],[10,21]],[[13,30],[4,28],[9,24],[17,28],[6,30],[4,15],[27,31],[4,28],[3,4],[7,31],[12,21],[6,21],[4,7],[10,15],[2,28],[17,23],[17,25],[7,28],[3,5],[23,27],[5,17],[4,10],[11,28],[4,10],[3,10],[3,10],[24,25],[2,8],[24,29],[0,1],[4,21],[9,28]],[[4,11],[13,24],[4,30],[3,4],[12,26],[11,18],[4,17],[19,24],[10,16],[3,10],[4,15],[18,23],[18,29],[1,30],[25,27],[10,30],[14,16],[11,12],[1,24],[3,23],[2,4],[10,26],[17,24],[1,13],[11,29],[5,9],[26,28],[4,15],[5,9],[3,9],[3,21],[9,26]],[[21,25],[10,22],[9,31],[2,29],[4,25],[10,26],[3,10],[1,4],[9,11],[10,24],[24,25],[3,13],[20,26],[10,28],[6,23],[10,14],[0,16],[4,24],[4,18],[11,13],[7,28],[4,10],[5,14],[18,28],[17,19],[4,9],[0,9],[2,28],[18,20],[2,26],[4,19],[11,26]],[[4,25],[6,9],[11,14],[3,4],[4,20],[0,9],[25,28],[13,19],[5,11],[9,15],[16,19],[7,8],[4,24],[3,4],[3,27],[3,4],[4,10],[1,10],[3,4],[12,26],[11,23],[26,28],[15,17],[4,6],[4,24],[13,26],[22,27],[9,11],[12,22],[3,20],[28,30],[11,23]],[[11,31],[10,23],[5,16],[14,28],[4,9],[4,20],[6,23],[13,24],[3,4],[6,8],[24,28],[11,15],[3,11],[13,24],[4,22],[9,21],[13,20],[5,27],[2,24],[19,25],[28,29],[9,17],[4,29],[4,9],[16,26],[9,21],[4,23],[8,29],[12,18],[8,11],[0,9],[22,24]],[[0,11],[1,16],[8,13],[12,23],[5,20],[1,29],[3,7],[3,17],[0,10],[2,5],[2,16],[17,29],[1,9],[5,28],[11,21],[5,7],[18,19],[3,16],[9,11],[20,24],[3,26],[1,6],[8,25],[5,9],[1,7],[16,31],[10,15],[9,31],[3,31],[2,9],[2,17],[3,24]],[[6,24],[4,27],[4,30],[9,26],[0,26],[16,20],[20,23],[7,26],[3,12],[2,7],[7,12],[4,27],[6,20],[16,27],[3,4],[4,20],[9,28],[4,26],[1,27],[3,8],[11,16],[17,21],[12,24],[9,27],[2,20],[0,18],[20,23],[4,16],[17,22],[9,11],[11,14],[10,14]],[[16,30],[0,8],[17,29],[5,9],[3,6],[4,9],[13,22],[1,17],[1,10],[0,25],[23,29],[4,28],[10,15],[4,22],[4,20],[14,25],[10,12],[4,23],[8,28],[10,18],[9,10],[4,26],[3,25],[11,19],[8,18],[7,15],[1,4],[11,27],[23,26],[9,20],[4,11],[16,27]],[[4,12],[12,25],[11,22],[4,25],[4,13],[9,26],[3,4],[11,25],[4,22],[19,29],[18,22],[9,16],[9,18],[6,15],[0,21],[15,16],[12,25],[10,28],[7,29],[10,28],[19,20],[0,5],[22,26],[4,13],[5,8],[14,27],[9,28],[18,28],[10,15],[17,26],[8,26],[1,10]],[[10,17],[22,24],[9,23],[14,24],[9,26],[0,29],[4,9],[14,17],[14,24],[10,17],[28,31],[3,16],[4,21],[12,27],[4,28],[2,13],[3,4],[17,27],[3,25],[15,24],[11,15],[0,10],[4,27],[4,17],[3,4],[0,9],[4,20],[22,29],[3,7],[10,17],[24,25],[23,27]],[[15,21],[7,23],[4,6],[10,24],[4,31],[24,27],[20,28],[3,11],[18,31],[3,20],[4,30],[4,9],[15,27],[16,28],[14,20],[16,29],[22,26],[9,17],[11,25],[25,30],[23,27],[18,21],[23,24],[25,27],[7,23],[4,30],[3,11],[3,21],[16,22],[10,26],[21,24],[4,21]],[[25,26],[4,8],[1,10],[16,23],[4,14],[4,11],[9,21],[11,29],[10,22],[5,24],[4,31],[21,24],[20,25],[1,4],[15,26],[18,24],[8,20],[6,10],[11,18],[22,23],[18,25],[4,13],[17,23],[9,30],[29,31],[11,29],[14,15],[4,12],[9,16],[15,24],[3,14],[9,22]],[[1,4],[11,17],[3,25],[3,23],[4,31],[0,24],[7,25],[1,30],[7,10],[3,9],[3,26],[7,16],[5,24],[4,10],[4,5],[9,11],[3,4],[3,7],[9,23],[6,17],[19,25],[12,24],[0,9],[8,11],[20,26],[4,10],[10,25],[5,7],[20,25],[11,30],[8,26],[9,10]],[[11,26],[3,4],[4,11],[25,30],[9,20],[4,5],[12,25],[23,31],[4,5],[2,11],[1,4],[12,16],[19,24],[5,7],[11,14],[4,28],[2,12],[4,20],[10,24],[13,28],[11,15],[10,25],[1,9],[9,30],[4,5],[1,24],[10,29],[16,25],[17,29],[4,10],[8,10],[3,26]],[[22,28],[9,12],[15,29],[9,10],[9,24],[12,23],[0,25],[4,14],[1,11],[9,19],[3,10],[3,7],[4,30],[24,29],[11,28],[10,18],[23,25],[4,28],[22,27],[21,30],[17,27],[4,9],[6,10],[0,28],[9,22],[4,12],[8,10],[19,28],[7,29],[2,21],[9,11],[4,14]],[[11,31],[4,23],[11,20],[11,26],[3,17],[23,28],[17,25],[6,22],[11,25],[0,21],[19,28],[4,9],[10,13],[12,24],[6,12],[4,5],[13,22],[4,22],[4,28],[4,26],[12,23],[7,23],[4,31],[9,17],[23,26],[4,10],[1,8],[3,28],[4,30],[27,31],[11,16],[9,30]],[[9,22],[5,26],[5,25],[9,17],[3,7],[21,27],[3,13],[4,16],[13,29],[9,29],[4,29],[4,10],[7,8],[21,25],[4,22],[10,22],[10,12],[3,8],[4,21],[4,8],[5,15],[10,12],[8,26],[1,3],[4,9],[5,17],[4,11],[0,14],[6,29],[22,29],[11,20],[8,25]],[[30,31],[4,11],[24,31],[4,11],[2,3],[9,17],[9,31],[2,21],[22,30],[4,10],[4,10],[7,22],[8,9],[4,25],[3,28],[7,19],[16,21],[3,4],[3,26],[0,27],[15,25],[1,3],[30,31],[2,10],[5,28],[21,28],[0,23],[14,28],[17,19],[9,21],[4,15],[1,17]],[[7,25],[23,28],[11,16],[9,15],[0,9],[4,21],[0,6],[1,4],[7,29],[3,11],[3,28],[4,26],[4,7],[15,22],[10,25],[3,27],[5,28],[5,9],[18,30],[4,22],[10,12],[4,17],[2,3],[7,9],[3,9],[9,17],[9,16],[18,30],[3,18],[7,11],[4,11],[4,24]],[[18,24],[24,31],[4,29],[10,30],[6,11],[5,11],[1,4],[3,7],[12,28],[14,29],[9,10],[9,28],[0,30],[15,27],[22,24],[10,17],[3,9],[0,9],[19,24],[16,18],[8,17],[3,4],[1,4],[1,17],[5,28],[11,27],[5,22],[30,31],[6,7],[10,29],[25,26],[0,9]],[[19,26],[18,24],[5,25],[10,13],[9,25],[23,31],[4,5],[20,26],[4,8],[16,23],[8,17],[1,3],[15,22],[4,9],[23,28],[8,11],[17,25],[10,12],[3,11],[24,25],[11,23],[24,27],[16,26],[4,17],[8,30],[3,11],[8,17],[1,7],[9,30],[9,28],[19,20],[10,19]],[[4,16],[10,15],[3,13],[17,28],[11,17],[4,29],[16,29],[4,22],[4,20],[5,8],[6,13],[3,10],[20,28],[3,9],[9,15],[4,12],[0,10],[18,30],[10,17],[11,19],[8,30],[11,14],[16,23],[9,11],[15,20],[3,16],[13,22],[4,11],[0,25],[0,17],[4,17],[4,27]],[[10,27],[7,30],[10,18],[6,18],[25,30],[5,8],[4,9],[3,17],[1,18],[3,4],[24,26],[18,25],[4,10],[23,27],[12,20],[3,18],[24,28],[7,10],[17,24],[24,29],[2,16],[4,23],[15,31],[0,17],[17,20],[7,10],[6,7],[3,13],[3,16],[0,30],[9,27],[4,25]],[[7,11],[10,11],[23,26],[2,4],[19,22],[25,29],[9,20],[11,29],[13,27],[13,17],[11,27],[10,23],[28,29],[4,8],[2,31],[3,5],[9,10],[10,17],[4,14],[5,23],[16,24],[7,10],[10,22],[3,4],[1,17],[9,24],[7,31],[8,25],[17,22],[0,4],[5,9],[4,12]],[[13,23],[12,16],[4,22],[24,25],[11,27],[9,28],[1,24],[4,29],[3,12],[7,24],[5,10],[6,31],[13,26],[9,23],[7,20],[4,28],[4,11],[10,18],[4,10],[17,18],[14,20],[10,20],[7,29],[3,4],[9,12],[10,17],[4,27],[1,30],[3,22],[17,29],[4,9],[3,4]],[[9,23],[0,8],[11,29],[8,17],[9,28],[4,22],[20,31],[5,22],[7,27],[4,24],[4,25],[10,30],[10,13],[16,25],[17,24],[10,23],[1,30],[3,9],[8,14],[11,28],[13,27],[13,28],[13,15],[8,10],[26,28],[1,31],[3,11],[4,29],[6,9],[4,26],[9,29],[10,17]],[[10,16],[26,30],[2,8],[9,21],[26,30],[10,20],[9,30],[4,13],[4,11],[16,17],[10,26],[10,25],[9,22],[7,28],[7,26],[24,30],[1,10],[0,10],[4,27],[11,19],[3,16],[24,31],[18,28],[11,17],[2,31],[4,12],[4,9],[10,30],[4,14],[8,21],[8,15],[4,9]],[[12,24],[10,29],[17,21],[10,17],[2,23],[15,21],[2,22],[10,21],[12,16],[9,23],[2,11],[3,16],[28,30],[14,15],[13,23],[22,25],[12,18],[9,28],[22,27],[29,30],[16,22],[12,18],[7,20],[16,25],[9,16],[5,17],[14,27],[17,29],[4,11],[4,26],[10,24],[11,29]],[[24,28],[8,20],[21,25],[3,30],[3,24],[4,17],[11,28],[2,10],[10,27],[7,26],[17,26],[19,27],[22,26],[3,22],[10,11],[20,30],[13,25],[14,25],[13,28],[28,30],[9,14],[9,19],[26,31],[4,25],[4,25],[3,10],[18,25],[3,31],[9,30],[4,10],[29,30],[7,14]],[[11,17],[12,14],[3,27],[4,9],[4,11],[4,11],[11,17],[4,16],[15,24],[16,17],[9,17],[12,26],[1,4],[9,30],[4,19],[17,22],[4,17],[8,24],[4,25],[6,18],[27,28],[13,29],[22,24],[15,21],[4,29],[0,20],[11,28],[2,31],[4,16],[4,26],[8,23],[23,25]]]
CAP = 64
def setup_inputs(rng):
    return {"x": rng.standard_normal((N, TOK, D), dtype=np.float32)}
def reference(x):
    y = np.full((N, CAP, D), np.nan, x.dtype)
    fill = [0] * N
    for r in range(N):
        for t in range(TOK):
            for e in ROUTE[r][t]:
                if fill[e] < CAP:
                    y[e][fill[e]] = x[r][t]
                    fill[e] += 1
    return {"y": y}

@@ -1,0 +1,158 @@
+from concourse import bass
+
+SCRATCH = {
+    "stage": ("dram", [32, 128, 4], "float32"),
+    "land": ("dram", [64, 128, 4], "float32"),
+}
+SEMAPHORES = ["loaded", "hand0", "hand1", "sent", "arrived", "stored"]
+
+OFF_CHIP_ENGINES = 8
+PAIR_PRICE = 10
+CACHE = {}
+
+
+def kept_copies(route, cap):
+    fill = [0] * len(route)
+    dest = []
+    for tokens in route:
+        rows = []
+        for experts in tokens:
+            keep = []
+            for e in experts:
+                if fill[e] < cap:
+                    keep.append((e, fill[e]))
+                    fill[e] += 1
+            rows.append(keep)
+        dest.append(rows)
+    return dest, fill
+
+
+def links(a, b):
+    if a == b:
+        return ()
+    if (a ^ b) & 1:
+        if b == a ^ 1:
+            return (("mate", a),)
+        return (("mate", a), ("out", a ^ 1), ("in", b))
+    return (("out", a), ("in", b))
+
+
+def split(dest, chips):
+    n = len(dest)
+    live = [[t for t, d in enumerate(dest[r]) if d] for r in range(n)]
+    way = [[[k for e, row in d for k in links(chips[r], chips[e])] for d in dest[r]] for r in range(n)]
+    side = [[None] * len(dest[r]) for r in range(n)]
+    load, used = {}, {}
+    for r in range(n):
+        for i, t in enumerate(live[r]):
+            s = side[r][t] = i & 1
+            for k in way[r][t]:
+                load[k, s] = load.get((k, s), 0) + 1
+                load.setdefault((k, 1 - s), 0)
+            for e, row in dest[r][t]:
+                used[r, e, s] = used.get((r, e, s), 0) + 1
+                used.setdefault((r, e, 1 - s), 0)
+
+    def flip(r, t):
+        s = side[r][t]
+        o = 1 - s
+        change = 0
+        for k in way[r][t]:
+            change += 2 * (load[k, o] - load[k, s]) + 2
+            load[k, s] -= 1
+            load[k, o] += 1
+        for e, row in dest[r][t]:
+            if used[r, e, s] == 1:
+                change -= PAIR_PRICE
+            if used[r, e, o] == 0:
+                change += PAIR_PRICE
+            used[r, e, s] -= 1
+            used[r, e, o] += 1
+        side[r][t] = o
+        return change
+
+    better = True
+    while better:
+        better = False
+        for r in range(n):
+            for a in live[r]:
+                for b in live[r]:
+                    if side[r][a] == 0 and side[r][b] == 1:
+                        if flip(r, a) + flip(r, b) < 0:
+                            better = True
+                        else:
+                            flip(r, a)
+                            flip(r, b)
+    return side
+
+
+def plan(T):
+    if "plan" not in CACHE:
+        dest, fill = kept_copies(T.tables["ROUTE"], T.tables["CAP"])
+        CACHE["plan"] = (dest, fill, split(dest, [c // 8 for c in T.cores]))
+    return CACHE["plan"]
+
+
+def helpers_of(rank_core, topo):
+    first = rank_core - rank_core % 8
+    other_parity = (first ^ 8) + rank_core % 8
+    found = {}
+    for c in range(first, first + 8):
+        if c != rank_core and topo.may_write(c, other_parity):
+            found.setdefault(topo.die(c), c)
+    return found
+
+
+def batches(rank, die, side):
+    mine = [t for t, s in enumerate(side[rank]) if s == die]
+    return mine[:OFF_CHIP_ENGINES], mine[OFF_CHIP_ENGINES:]
+
+
+def rank_program(g, core, T, topo):
+    dest, fill, side = plan(T)
+    hand = (T.sem.hand0, T.sem.hand1)
+    rank = T.rank_of(core)
+
+    if rank is not None:
+        helpers = helpers_of(core, topo)
+        g.dma_start(T.stage[:], T.x[:]).then_inc(T.sem.loaded, 16)
+        g.wait_ge(T.sem.loaded, 16)
+        handed = 0
+        for b in (0, 1):
+            call = []
+            for die, helper in sorted(helpers.items()):
+                rid, pid = topo.addr(helper, core)
+                for t in batches(rank, die, side)[b]:
+                    call.append(bass.RemoteDMATransfer(dst_ids=[bass.DstId(rid=rid, pnc=pid)], dma_engine_mask=1 << len(call),
+                                                       remote_sem=hand[b], srcs=[T.stage[t]], dsts=[T.stage[t]]))
+            if call:
+                g.remote_dma_fused(call, local_sem=T.sem.sent)
+                handed += len(call)
+        if handed:
+            g.wait_ge(T.sem.sent, handed)
+        if fill[rank]:
+            g.wait_ge(T.sem.arrived, fill[rank])
+            g.dma_start(T.y[0:fill[rank]], T.land[0:fill[rank]]).then_inc(T.sem.stored, 16)
+            g.wait_ge(T.sem.stored, 16)
+        return
+
+    for owner in T.cores:
+        if owner // 8 == core // 8 and helpers_of(owner, topo).get(topo.die(core)) == core:
+            rank = T.rank_of(owner)
+            left = 0
+            for b, tokens in enumerate(batches(rank, topo.die(core), side)):
+                if not tokens:
+                    continue
+                g.wait_ge(hand[b], len(tokens))
+                call = []
+                for t in tokens:
+                    ids = []
+                    for e, row in dest[rank][t]:
+                        rid, pid = topo.addr(T.cores[e], core)
+                        ids.append(bass.DstId(rid=rid, pnc=pid))
+                    call.append(bass.RemoteDMATransfer(dst_ids=ids, dma_engine_mask=1 << len(call), remote_sem=T.sem.arrived,
+                                                       srcs=[T.stage[t]], dsts=[T.land[row] for e, row in dest[rank][t]]))
+                g.remote_dma_fused(call, local_sem=T.sem.sent)
+                left += len(call)
+            if left:
+                g.wait_ge(T.sem.sent, left)

@@ -4,10 +4,10 @@ SCRATCH = {
     "stage": ("dram", [32, 128, 4], "float32"),
     "land": ("dram", [64, 128, 4], "float32"),
 }
-SEMAPHORES = ["loaded", "hand0", "hand1", "sent", "arrived", "stored"]
+SEMAPHORES = ["local", "sent", "arrived"]
 
 OFF_CHIP_ENGINES = 8
-PAIR_PRICE = 10
+MIRROR = 7
 CACHE = {}
 
 
@@ -27,132 +27,53 @@ def kept_copies(route, cap):
     return dest, fill
 
 
-def links(a, b):
-    if a == b:
-        return ()
-    if (a ^ b) & 1:
-        if b == a ^ 1:
-            return (("mate", a),)
-        return (("mate", a), ("out", a ^ 1), ("in", b))
-    return (("out", a), ("in", b))
-
-
-def split(dest, chips):
-    n = len(dest)
-    live = [[t for t, d in enumerate(dest[r]) if d] for r in range(n)]
-    way = [[[k for e, row in d for k in links(chips[r], chips[e])] for d in dest[r]] for r in range(n)]
-    side = [[None] * len(dest[r]) for r in range(n)]
-    load, used = {}, {}
-    for r in range(n):
-        for i, t in enumerate(live[r]):
-            s = side[r][t] = i & 1
-            for k in way[r][t]:
-                load[k, s] = load.get((k, s), 0) + 1
-                load.setdefault((k, 1 - s), 0)
-            for e, row in dest[r][t]:
-                used[r, e, s] = used.get((r, e, s), 0) + 1
-                used.setdefault((r, e, 1 - s), 0)
-
-    def flip(r, t):
-        s = side[r][t]
-        o = 1 - s
-        change = 0
-        for k in way[r][t]:
-            change += 2 * (load[k, o] - load[k, s]) + 2
-            load[k, s] -= 1
-            load[k, o] += 1
-        for e, row in dest[r][t]:
-            if used[r, e, s] == 1:
-                change -= PAIR_PRICE
-            if used[r, e, o] == 0:
-                change += PAIR_PRICE
-            used[r, e, s] -= 1
-            used[r, e, o] += 1
-        side[r][t] = o
-        return change
-
-    better = True
-    while better:
-        better = False
-        for r in range(n):
-            for a in live[r]:
-                for b in live[r]:
-                    if side[r][a] == 0 and side[r][b] == 1:
-                        if flip(r, a) + flip(r, b) < 0:
-                            better = True
-                        else:
-                            flip(r, a)
-                            flip(r, b)
-    return side
-
-
 def plan(T):
     if "plan" not in CACHE:
-        dest, fill = kept_copies(T.tables["ROUTE"], T.tables["CAP"])
-        CACHE["plan"] = (dest, fill, split(dest, [c // 8 for c in T.cores]))
+        CACHE["plan"] = kept_copies(T.tables["ROUTE"], T.tables["CAP"])
     return CACHE["plan"]
 
 
-def helpers_of(rank_core, topo):
-    first = rank_core - rank_core % 8
-    other_parity = (first ^ 8) + rank_core % 8
-    found = {}
-    for c in range(first, first + 8):
-        if c != rank_core and topo.may_write(c, other_parity):
-            found.setdefault(topo.die(c), c)
-    return found
-
-
-def batches(rank, die, side):
-    mine = [t for t, s in enumerate(side[rank]) if s == die]
-    return mine[:OFF_CHIP_ENGINES], mine[OFF_CHIP_ENGINES:]
-
-
 def rank_program(g, core, T, topo):
-    dest, fill, side = plan(T)
-    hand = (T.sem.hand0, T.sem.hand1)
+    dest, fill = plan(T)
     rank = T.rank_of(core)
 
-    if rank is not None:
-        helpers = helpers_of(core, topo)
-        g.dma_start(T.stage[:], T.x[:]).then_inc(T.sem.loaded, 16)
-        g.wait_ge(T.sem.loaded, 16)
-        handed = 0
-        for b in (0, 1):
-            call = []
-            for die, helper in sorted(helpers.items()):
-                rid, pid = topo.addr(helper, core)
-                for t in batches(rank, die, side)[b]:
-                    call.append(bass.RemoteDMATransfer(dst_ids=[bass.DstId(rid=rid, pnc=pid)], dma_engine_mask=1 << len(call),
-                                                       remote_sem=hand[b], srcs=[T.stage[t]], dsts=[T.stage[t]]))
-            if call:
-                g.remote_dma_fused(call, local_sem=T.sem.sent)
-                handed += len(call)
-        if handed:
-            g.wait_ge(T.sem.sent, handed)
-        if fill[rank]:
-            g.wait_ge(T.sem.arrived, fill[rank])
-            g.dma_start(T.y[0:fill[rank]], T.land[0:fill[rank]]).then_inc(T.sem.stored, 16)
-            g.wait_ge(T.sem.stored, 16)
+    if rank is None:
+        owners = [c for c in T.cores if c // 8 == core // 8]
+        if core % 8 != MIRROR or not owners:
+            return
+        rank = T.rank_of(owners[0])
+        own = [(t, row) for t, d in enumerate(dest[rank]) for e, row in d if e == rank]
+        if not own:
+            return
+        g.wait_ge(T.sem.arrived, len(own))
+        rid, pid = topo.addr(owners[0], core)
+        call = [bass.RemoteDMATransfer(dst_ids=[bass.DstId(rid=rid, pnc=pid)], dma_engine_mask=1 << i, remote_sem=T.sem.arrived,
+                                       srcs=[T.stage[t]], dsts=[T.land[row]]) for i, (t, row) in enumerate(own)]
+        g.remote_dma_fused(call, local_sem=T.sem.sent)
+        g.wait_ge(T.sem.sent, len(call))
         return
 
-    for owner in T.cores:
-        if owner // 8 == core // 8 and helpers_of(owner, topo).get(topo.die(core)) == core:
-            rank = T.rank_of(owner)
-            left = 0
-            for b, tokens in enumerate(batches(rank, topo.die(core), side)):
-                if not tokens:
-                    continue
-                g.wait_ge(hand[b], len(tokens))
-                call = []
-                for t in tokens:
-                    ids = []
-                    for e, row in dest[rank][t]:
-                        rid, pid = topo.addr(T.cores[e], core)
-                        ids.append(bass.DstId(rid=rid, pnc=pid))
-                    call.append(bass.RemoteDMATransfer(dst_ids=ids, dma_engine_mask=1 << len(call), remote_sem=T.sem.arrived,
-                                                       srcs=[T.stage[t]], dsts=[T.land[row] for e, row in dest[rank][t]]))
-                g.remote_dma_fused(call, local_sem=T.sem.sent)
-                left += len(call)
-            if left:
-                g.wait_ge(T.sem.sent, left)
+    mirror = core - core % 8 + MIRROR
+    live = [t for t, d in enumerate(dest[rank]) if d]
+    home = {t: any(e == rank for e, row in dest[rank][t]) for t in live}
+    order = sorted(live, key=lambda t: (not home[t], -max(fill[e] for e, row in dest[rank][t]), t))
+
+    g.dma_start(T.stage[:], T.x[:]).then_inc(T.sem.local, 16)
+    g.wait_ge(T.sem.local, 16)
+    for i in range(0, len(order), OFF_CHIP_ENGINES):
+        call = []
+        for t in order[i:i + OFF_CHIP_ENGINES]:
+            ids, dsts = [], []
+            for e, row in dest[rank][t]:
+                rid, pid = topo.addr(T.cores[e] if e != rank else mirror, core)
+                ids.append(bass.DstId(rid=rid, pnc=pid))
+                dsts.append(T.land[row] if e != rank else T.stage[t])
+            call.append(bass.RemoteDMATransfer(dst_ids=ids, dma_engine_mask=1 << len(call), remote_sem=T.sem.arrived,
+                                               srcs=[T.stage[t]], dsts=dsts))
+        g.remote_dma_fused(call, local_sem=T.sem.sent)
+    if fill[rank]:
+        g.wait_ge(T.sem.arrived, fill[rank])
+        g.dma_start(T.y[0:fill[rank]], T.land[0:fill[rank]]).then_inc(T.sem.local, 16)
+        g.wait_ge(T.sem.local, 32)
+    if order:
+        g.wait_ge(T.sem.sent, len(order))

@@ -7,7 +7,7 @@ SCRATCH = {
 SEMAPHORES = ["local", "sent", "arrived"]
 
 OFF_CHIP_ENGINES = 8
-MIRROR = 7
+MIRRORS = (7, 5, 4)
 CACHE = {}
 
 
@@ -33,16 +33,25 @@ def plan(T):
     return CACHE["plan"]
 
 
+def way(a, b):
+    if a == b:
+        return 4
+    if (a ^ b) & 1:
+        return 1 if b == a ^ 1 else 3
+    return 2
+
+
 def rank_program(g, core, T, topo):
     dest, fill = plan(T)
     rank = T.rank_of(core)
 
     if rank is None:
         owners = [c for c in T.cores if c // 8 == core // 8]
-        if core % 8 != MIRROR or not owners:
+        if core % 8 not in MIRRORS or not owners:
             return
         rank = T.rank_of(owners[0])
         own = [(t, row) for t, d in enumerate(dest[rank]) for e, row in d if e == rank]
+        own = own[MIRRORS.index(core % 8)::len(MIRRORS)]
         if not own:
             return
         g.wait_ge(T.sem.arrived, len(own))
@@ -53,10 +62,13 @@ def rank_program(g, core, T, topo):
         g.wait_ge(T.sem.sent, len(call))
         return
 
-    mirror = core - core % 8 + MIRROR
-    live = [t for t, d in enumerate(dest[rank]) if d]
-    home = {t: any(e == rank for e, row in dest[rank][t]) for t in live}
-    order = sorted(live, key=lambda t: (not home[t], -max(fill[e] for e, row in dest[rank][t]), t))
+    def length(e):
+        return way(core // 8, T.cores[e] // 8)
+
+    own = [t for t, d in enumerate(dest[rank]) for e, row in d if e == rank]
+    mirror = {t: core - core % 8 + MIRRORS[i % len(MIRRORS)] for i, t in enumerate(own)}
+    copies = {t: sorted(d, key=lambda p: -length(p[0])) for t, d in enumerate(dest[rank]) if d}
+    order = sorted(copies, key=lambda t: (-length(copies[t][0][0]), -max(fill[e] for e, row in copies[t]), t))
 
     g.dma_start(T.stage[:], T.x[:]).then_inc(T.sem.local, 16)
     g.wait_ge(T.sem.local, 16)
@@ -64,8 +76,8 @@ def rank_program(g, core, T, topo):
         call = []
         for t in order[i:i + OFF_CHIP_ENGINES]:
             ids, dsts = [], []
-            for e, row in dest[rank][t]:
-                rid, pid = topo.addr(T.cores[e] if e != rank else mirror, core)
+            for e, row in copies[t]:
+                rid, pid = topo.addr(T.cores[e] if e != rank else mirror[t], core)
                 ids.append(bass.DstId(rid=rid, pnc=pid))
                 dsts.append(T.land[row] if e != rank else T.stage[t])
             call.append(bass.RemoteDMATransfer(dst_ids=ids, dma_engine_mask=1 << len(call), remote_sem=T.sem.arrived,

@@ -35,10 +35,8 @@ def plan(T):
 
 def way(a, b):
     if a == b:
-        return 4
-    if (a ^ b) & 1:
-        return 1 if b == a ^ 1 else 3
-    return 2
+        return 3
+    return 2 if (a ^ b) & 1 and b != a ^ 1 else 1
 
 
 def rank_program(g, core, T, topo):

from concourse import bass

SCRATCH = {
    "stage": ("dram", [32, 128, 4], "float32"),
    "land": ("dram", [64, 128, 4], "float32"),
}
SEMAPHORES = ["local", "sent", "arrived"]

OFF_CHIP_ENGINES = 8
MIRRORS = (7, 5, 4)
CACHE = {}


def kept_copies(route, cap):
    fill = [0] * len(route)
    dest = []
    for tokens in route:
        rows = []
        for experts in tokens:
            keep = []
            for e in experts:
                if fill[e] < cap:
                    keep.append((e, fill[e]))
                    fill[e] += 1
            rows.append(keep)
        dest.append(rows)
    return dest, fill


def plan(T):
    if "plan" not in CACHE:
        CACHE["plan"] = kept_copies(T.tables["ROUTE"], T.tables["CAP"])
    return CACHE["plan"]


def way(a, b):
    if a == b:
        return 3
    return 2 if (a ^ b) & 1 and b != a ^ 1 else 1


def rank_program(g, core, T, topo):
    dest, fill = plan(T)
    rank = T.rank_of(core)

    if rank is None:
        owners = [c for c in T.cores if c // 8 == core // 8]
        if core % 8 not in MIRRORS or not owners:
            return
        rank = T.rank_of(owners[0])
        own = [(t, row) for t, d in enumerate(dest[rank]) for e, row in d if e == rank]
        own = own[MIRRORS.index(core % 8)::len(MIRRORS)]
        if not own:
            return
        g.wait_ge(T.sem.arrived, len(own))
        rid, pid = topo.addr(owners[0], core)
        call = [bass.RemoteDMATransfer(dst_ids=[bass.DstId(rid=rid, pnc=pid)], dma_engine_mask=1 << i, remote_sem=T.sem.arrived,
                                       srcs=[T.stage[t]], dsts=[T.land[row]]) for i, (t, row) in enumerate(own)]
        g.remote_dma_fused(call, local_sem=T.sem.sent)
        g.wait_ge(T.sem.sent, len(call))
        return

    def length(e):
        return way(core // 8, T.cores[e] // 8)

    own = [t for t, d in enumerate(dest[rank]) for e, row in d if e == rank]
    mirror = {t: core - core % 8 + MIRRORS[i % len(MIRRORS)] for i, t in enumerate(own)}
    copies = {t: sorted(d, key=lambda p: -length(p[0])) for t, d in enumerate(dest[rank]) if d}
    order = sorted(copies, key=lambda t: (-length(copies[t][0][0]), -max(fill[e] for e, row in copies[t]), t))

    g.dma_start(T.stage[:], T.x[:]).then_inc(T.sem.local, 16)
    g.wait_ge(T.sem.local, 16)
    for i in range(0, len(order), OFF_CHIP_ENGINES):
        call = []
        for t in order[i:i + OFF_CHIP_ENGINES]:
            ids, dsts = [], []
            for e, row in copies[t]:
                rid, pid = topo.addr(T.cores[e] if e != rank else mirror[t], core)
                ids.append(bass.DstId(rid=rid, pnc=pid))
                dsts.append(T.land[row] if e != rank else T.stage[t])
            call.append(bass.RemoteDMATransfer(dst_ids=ids, dma_engine_mask=1 << len(call), remote_sem=T.sem.arrived,
                                               srcs=[T.stage[t]], dsts=dsts))
        g.remote_dma_fused(call, local_sem=T.sem.sent)
    if fill[rank]:
        g.wait_ge(T.sem.arrived, fill[rank])
        g.dma_start(T.y[0:fill[rank]], T.land[0:fill[rank]]).then_inc(T.sem.local, 16)
        g.wait_ge(T.sem.local, 32)
    if order:
        g.wait_ge(T.sem.sent, len(order))
